import numpy as np
import ml_dtypes


def mxq(x, axis, fmt="e4m3"):
    dtype, down = {"e4m3": (ml_dtypes.float8_e4m3fn, 7), "e5m2": (ml_dtypes.float8_e5m2, 14)}[fmt]
    v = np.moveaxis(np.asarray(x, np.float32).astype(ml_dtypes.bfloat16).astype(np.float64), axis, -1)
    blocks = v.reshape(v.shape[:-1] + (-1, 32))
    amax = np.abs(blocks).max(-1, keepdims=True)
    byte = np.maximum(np.where(amax > 0, np.frexp(amax)[1] - 1 + 127, 0) - down, 1)
    scale = np.exp2(byte - 127.0)
    codes = (blocks / scale).astype(np.float32).astype(dtype).astype(np.float64)
    return np.moveaxis((codes * scale).reshape(v.shape), -1, axis)


WIDE = False


def mx_kscale(k):
    if not WIDE:
        return np.ones(k)
    levels = np.array([30, -30])
    if k % 512:
        return np.exp2(np.random.permutation(np.resize(levels, k // 32))).repeat(32)
    a = np.empty((k // 512, 16))
    for p in range(k // 512):
        a[p, :8] = np.random.permutation(np.resize(levels, 8))
        for g in range(8):
            far = levels[np.abs(levels - a[p, g]) >= 10]
            a[p, g + 8] = far[np.random.randint(len(far))]
    return np.exp2(a.ravel()).repeat(32)


def f64(x):
    return np.asarray(x).astype(np.float64)


def striped(idx):
    return np.tile(np.asarray(idx).reshape(-1, 16).T, (8, 1)).astype(np.uint16)


def unstriped(offs):
    return offs[:16].T.reshape(-1).astype(np.int64)


E2M1 = np.array([0.0, 0.5, 1.0, 1.5, 2.0, 3.0, 4.0, 6.0, -0.0, -0.5, -1.0, -1.5, -2.0, -3.0, -4.0, -6.0])


def pack_weight(w, fmt):
    k, n = w.shape
    w = f64(np.asarray(w, np.float32).astype(ml_dtypes.bfloat16)).reshape(k // 32, 32, n)
    amax = np.abs(w).max(1)
    if fmt == "e4m3":
        byte = np.frexp(amax)[1] - 1 + 127 - 7
    else:
        mant, ex = np.frexp(amax / 6.0)
        byte = np.where(mant > 0.5, ex, ex - 1) + 127
    byte = np.clip(np.where(amax > 0, byte, 1), 1, 254)
    scaled = (w * np.exp2(127.0 - byte)[:, None, :]).reshape(k, n).astype(np.float32)
    by_word = np.ascontiguousarray(scaled.reshape(k // 512, 128, 4, n).transpose(0, 1, 3, 2))
    if fmt == "e4m3":
        words = by_word.astype(ml_dtypes.float8_e4m3fn).view(np.uint8)
    else:
        c = by_word.astype(ml_dtypes.float4_e2m1fn).view(np.uint8) & 0xF
        words = (c[..., 0::2] | (c[..., 1::2] << 4)).reshape(k // 512, 128, 2 * n)
    return np.ascontiguousarray(words), np.ascontiguousarray(byte.astype(np.uint8).reshape(k // 512, 16, n))


def unpack_weight(words, scales, fmt):
    g, _, n = scales.shape
    words = np.ascontiguousarray(words).reshape(g, 128, n, -1)
    if fmt == "e4m3":
        vals = words.view(ml_dtypes.float8_e4m3fn).astype(np.float64)
    else:
        nib = np.empty((g, 128, n, 4), np.uint8)
        nib[..., 0::2] = words & 0xF
        nib[..., 1::2] = words >> 4
        vals = E2M1[nib]
    vals = vals * np.repeat(np.exp2(scales.astype(np.float64) - 127.0), 8, axis=1)[..., None]
    return vals.transpose(0, 1, 3, 2).reshape(g * 512, n)


K, F, T, Z, J, R, N, S, E = 512, 512, 1024, 1024, 256, 512, 256, 1024, 1024


def setup_inputs():
    n = np.random.standard_normal
    idx = np.random.permutation(T)[:J]
    idx2 = np.random.permutation(Z)[:J]
    idx3 = np.random.permutation(J)[:J]
    idx4 = np.random.permutation(S)[:N]
    idx5 = np.random.permutation(E)[:J]
    fk = mx_kscale(K)
    fr = mx_kscale(R)
    ff = mx_kscale(F)
    xtp = pack_weight(n((K, T)) / fk[:, None], "e2m1")
    wp = pack_weight(n((K, R)) * 1 / np.sqrt(K) * fk[:, None] * fr, "e4m3")
    xop = pack_weight(n((F, Z)) / ff[:, None], "e4m3")
    w0p = pack_weight(n((F, R)) * 1 / np.sqrt(F) * ff[:, None] * fr, "e2m1")
    vsp = pack_weight(n((R, S)) * 1 / np.sqrt(R) / fr[:, None], "e2m1")
    return {
        "xt_words": xtp[0],
        "xt_scales": xtp[1],
        "w_words": wp[0],
        "w_scales": wp[1],
        "xo_words": xop[0],
        "xo_scales": xop[1],
        "w0_words": w0p[0],
        "w0_scales": w0p[1],
        "sa": (np.random.uniform(0.5, 1.6, (R, 1))).astype(np.float32),
        "vs_words": vsp[0],
        "vs_scales": vsp[1],
        "offs": striped(idx),
        "offs2": striped(idx2),
        "offs3": striped(idx3),
        "offs4": striped(idx4),
        "offs5": striped(idx5),
    }


def reference(xt_words, xt_scales, w_words, w_scales, xo_words, xo_scales, w0_words, w0_scales, sa, vs_words, vs_scales, offs, offs2, offs3, offs4, offs5):
    idx = unstriped(offs)
    idx2 = unstriped(offs2)
    idx3 = unstriped(offs3)
    idx4 = unstriped(offs4)
    idx5 = unstriped(offs5)
    xtu = unpack_weight(xt_words, xt_scales, "e2m1")
    wu = unpack_weight(w_words, w_scales, "e4m3")
    xou = unpack_weight(xo_words, xo_scales, "e4m3")
    w0u = unpack_weight(w0_words, w0_scales, "e2m1")
    vsu = unpack_weight(vs_words, vs_scales, "e2m1")
    xtidxg = xtu[:, idx]
    xoidx2g = xou[:, idx2]
    a = wu.T @ xtidxg + w0u.T @ xoidx2g
    hid = np.abs(a - a[:, idx3] * f64(sa))
    vsidx4g = vsu[:, idx4]
    hidq = mxq(hid, 0, "e5m2")
    p = vsidx4g.T @ hidq
    y = np.zeros((N, E))
    y[:, idx5] = p
    return y

@@ -1,0 +1,187 @@
+from contextlib import ExitStack
+
+import concourse.mybir as mybir
+
+K, T, J, R, N, E = 512, 1024, 256, 512, 256, 1024
+FLOPS = 2 * (2 * K * R * J + R * N * J)
+
+F32 = mybir.dt.float32
+BF16 = mybir.dt.bfloat16
+I32 = mybir.dt.int32
+U32 = mybir.dt.uint32
+U16 = mybir.dt.uint16
+U8 = mybir.dt.uint8
+E4M3 = mybir.dt.float8_e4m3fn_x4
+E5M2 = mybir.dt.float8_e5m2_x4
+E2M1 = mybir.dt.float4_e2m1fn_x4
+ACT = mybir.ActivationFunctionType
+ALU = mybir.AluOpType
+
+P = 128
+PACK = 4
+HALF = J // 2
+
+
+def tile_list_lessneighbour_bank_store_scattered_kernel(
+    tc, xt_words, xt_scales, w_words, w_scales, xo_words, xo_scales, w0_words, w0_scales, sa,
+    vs_words, vs_scales, offs, offs2, offs3, offs4, offs5, out,
+):
+    nc = tc.nc
+    with ExitStack() as ctx:
+        sb = ctx.enter_context(tc.tile_pool(name="sb", bufs=1))
+        ps = ctx.enter_context(tc.psum_pool(name="ps", bufs=1))
+
+        def tile(name, shape, dtype):
+            return sb.tile(shape, dtype, name=name, align_bytes=64)
+
+        lists = {}
+
+        def load_list(name, src):
+            lists[name] = tile(name, [P, J // 16], U16)
+            nc.sync.dma_start(lists[name][:], src)
+
+        def load_words(queue, name, src, cols, dtype):
+            t = tile(name, [P, cols], dtype)
+            queue.dma_start(t[:].bitcast(I32), src.bitcast(I32))
+            return t
+
+        def plane_tile(name, cols, base):
+            t = tile(name, [P, 2 * cols], U8)
+            nc.vector.memset(t[:].bitcast(I32)[base : base + 64, :], 0)
+            return t
+
+        def load_plane(queue, t, src, base):
+            rows = src[0].bitcast(I32).rearrange("(b q r) n -> q r b n", b=2, q=2)
+            for q in range(2):
+                dst = t[:].bitcast(I32)[base + 32 * q : base + 32 * q + 4, :]
+                queue.dma_start(dst.rearrange("p (b n) -> p b n", b=2), rows[q])
+
+        def fold_plane(t, cols, base):
+            t32 = t[:].bitcast(I32)
+            c = cols // 4
+            if base == 0:
+                nc.vector.tensor_copy(t32[64:128, 0:c], t32[0:64, c : 2 * c])
+                return t[:, 0:cols]
+            nc.vector.tensor_copy(t32[0:64, c : 2 * c], t32[64:128, 0:c])
+            return t[:, cols : 2 * cols]
+
+        def window_plane(name, t, cols, base):
+            win = tile(name, [P, cols], U8)
+            t32, w32 = t[:].bitcast(I32), win[:].bitcast(I32)
+            c = cols // 4
+            for b in range(2):
+                nc.vector.tensor_copy(w32[64 * b : 64 * b + 64, :], t32[base : base + 64, c * b : c * (b + 1)])
+            return win[:]
+
+        def gather(name, window, idx, dtype):
+            g = tile(name, [P, J], dtype)
+            nc.vector.tensor_copy(g[:], window.indirect(idx[:]))
+            return g
+
+        xt_p = plane_tile("xt_p", T, 0)
+        w_p = plane_tile("w_p", R, 64)
+        xo_p = plane_tile("xo_p", T, 64)
+        w0_p = plane_tile("w0_p", R, 0)
+        vs_p = tile("vs_p", [P, T], U8)
+        nc.vector.memset(vs_p[:].bitcast(I32), 0)
+        pages = [tile("page%d" % i, [P, E], F32) for i in range(2)]
+        for page in pages:
+            nc.vector.memset(page[:], 0.0)
+
+        load_list("offs", offs)
+        xt_w = load_words(nc.sync, "xt_w", xt_words[0], T, U16)
+        w_w = load_words(nc.sync, "w_w", w_words[0].rearrange("p c r -> p (c r)"), R, U32)
+        xo_w = load_words(nc.sync, "xo_w", xo_words[0].rearrange("p c r -> p (c r)"), T, U32)
+        load_plane(nc.scalar, xt_p, xt_scales, 0)
+        load_plane(nc.scalar, w_p, w_scales, 64)
+        load_list("offs2", offs2)
+        w0_w = load_words(nc.sync, "w0_w", w0_words[0], R, U16)
+        load_list("offs4", offs4)
+        vs_w = load_words(nc.sync, "vs_w", vs_words[0], T, U16)
+        load_plane(nc.scalar, xo_p, xo_scales, 64)
+        load_plane(nc.scalar, w0_p, w0_scales, 0)
+        load_list("offs3", offs3)
+        sa_t = tile("sa_t", [P, PACK], F32)
+        nc.sync.dma_start(sa_t[:], sa.rearrange("(p t) o -> p (t o)", t=PACK))
+        vs_rows = vs_scales[0].bitcast(I32)
+        for q in range(4):
+            nc.sync.dma_start(vs_p[:].bitcast(I32)[32 * q : 32 * q + 4, :], vs_rows[4 * q : 4 * q + 4, :])
+        load_list("offs5", offs5)
+
+        def deal(engine_copy, name, src, dtype):
+            d = tile(name, [P, PACK, P], dtype)
+            view = src.rearrange("p (m t) -> p t m", t=PACK)
+            for t in range(0, PACK, 2):
+                engine_copy(d[:, t : t + 2, :], view[:, t : t + 2, :])
+            return d
+
+        acc = [ps.tile([P, J], F32, name="acc%d" % t) for t in range(PACK)]
+
+        xt_win = window_plane("xt_win", xt_p, T, 0)
+        w_win = fold_plane(w_p, R, 64)
+        w_sd = deal(nc.gpsimd.tensor_copy, "w_sd", w_win, U8)
+        w_d = deal(nc.scalar.copy, "w_d", w_w[:], U32)
+        xt_gs = gather("xt_gs", xt_win, lists["offs"], U8)
+        xt_g = gather("xt_g", xt_w[:], lists["offs"], U16)
+        for t in range(PACK):
+            nc.tensor.matmul_mx(
+                out=acc[t][:], lhsT=w_d[:, t, :].bitcast(E4M3), lhsT_scale=w_sd[:, t, :],
+                rhs=xt_g[:].bitcast(E2M1), rhs_scale=xt_gs[:], start=True, stop=False,
+            )
+
+        xo_g = gather("xo_g", xo_w[:], lists["offs2"], U32)
+        w0_win = fold_plane(w0_p, R, 0)
+        xo_win = window_plane("xo_win", xo_p, T, 64)
+        w0_sd = deal(nc.gpsimd.tensor_copy, "w0_sd", w0_win, U8)
+        w0_d = deal(nc.scalar.copy, "w0_d", w0_w[:], U16)
+        xo_gs = gather("xo_gs", xo_win, lists["offs2"], U8)
+        for t in range(PACK):
+            nc.tensor.matmul_mx(
+                out=acc[t][:], lhsT=w0_d[:, t, :].bitcast(E2M1), lhsT_scale=w0_sd[:, t, :],
+                rhs=xo_g[:].bitcast(E4M3), rhs_scale=xo_gs[:], start=False, stop=True,
+            )
+
+        vs_g = gather("vs_g", vs_w[:], lists["offs4"], U16)
+
+        a = []
+        for t in range(PACK):
+            a.append(tile("a%d" % t, [P, J], F32))
+            nc.vector.tensor_copy(a[t][:], acc[t][:])
+
+        diffs = []
+        for h in range(2):
+            part = lists["offs3"][:, 8 * h : 8 * h + 8]
+            diff = tile("diff%d" % h, [P, PACK, HALF], F32)
+            for t in range(PACK):
+                g = tile("g%d_%d" % (h, t), [P, HALF], F32)
+                nc.scalar.activation(out=g[:], in_=a[t][:].indirect(part), func=ACT.Copy, scale=sa_t[:, t : t + 1])
+                nc.vector.tensor_tensor(diff[:, t, :], acc[t][:, HALF * h : HALF * (h + 1)], g[:], ALU.subtract)
+            diffs.append(diff)
+            if h == 0:
+                vs_gs = gather("vs_gs", vs_p[:], lists["offs4"], U8)
+
+        hids = []
+        for h in range(2):
+            hid = tile("hid%d" % h, [P, HALF, PACK], BF16)
+            nc.scalar.activation(out=hid[:], in_=diffs[h][:].rearrange("p t j -> p j t"), func=ACT.Abs)
+            hids.append(hid)
+
+        for h in range(2):
+            hq = tile("hq%d" % h, [P, HALF], U32)
+            hs = tile("hs%d" % h, [P, HALF], U8)
+            nc.vector.quantize_mx(out=hq[:].bitcast(E5M2), scales=hs[:], in_=hids[h][:].rearrange("p j t -> p (j t)"))
+            part = lists["offs5"][:, 8 * h : 8 * h + 8]
+            res = []
+            for i in (1, 0):
+                prod = ps.tile([P, HALF], F32, name="prod%d_%d" % (h, i))
+                nc.tensor.matmul_mx(
+                    out=prod[:], lhsT=vs_g[:, P * i : P * (i + 1)].bitcast(E2M1), lhsT_scale=vs_gs[:, P * i : P * (i + 1)],
+                    rhs=hq[:].bitcast(E5M2), rhs_scale=hs[:], start=True, stop=True,
+                )
+                res.append(tile("res%d_%d" % (h, i), [P, HALF], F32))
+                nc.vector.tensor_copy(res[-1][:], prod[:])
+            nc.scalar.activation(out=pages[1][:].indirect(part), in_=res[0][:], func=ACT.Copy)
+            nc.vector.tensor_copy(pages[0][:].indirect(part), res[1][:])
+
+        nc.sync.dma_start(out[0:P, :], pages[0][:])
+        nc.scalar.dma_start(out[P : 2 * P, :], pages[1][:])

@@ -31,8 +31,8 @@ def tile_list_lessneighbour_bank_store_scattered_kernel(
         sb = ctx.enter_context(tc.tile_pool(name="sb", bufs=1))
         ps = ctx.enter_context(tc.psum_pool(name="ps", bufs=1))
 
-        def tile(name, shape, dtype):
-            return sb.tile(shape, dtype, name=name, align_bytes=64)
+        def tile(name, shape, dtype, tag=None):
+            return sb.tile(shape, dtype, name=name, tag=tag or name, align_bytes=64)
 
         lists = {}
 
@@ -50,11 +50,10 @@ def tile_list_lessneighbour_bank_store_scattered_kernel(
             nc.vector.memset(t[:].bitcast(I32)[base : base + 64, :], 0)
             return t
 
-        def load_plane(queue, t, src, base):
+        def load_plane(queue, t, src, base, q):
             rows = src[0].bitcast(I32).rearrange("(b q r) n -> q r b n", b=2, q=2)
-            for q in range(2):
-                dst = t[:].bitcast(I32)[base + 32 * q : base + 32 * q + 4, :]
-                queue.dma_start(dst.rearrange("p (b n) -> p b n", b=2), rows[q])
+            dst = t[:].bitcast(I32)[base + 32 * q : base + 32 * q + 4, :]
+            queue.dma_start(dst.rearrange("p (b n) -> p b n", b=2), rows[q])
 
         def fold_plane(t, cols, base):
             t32 = t[:].bitcast(I32)
@@ -80,29 +79,29 @@ def tile_list_lessneighbour_bank_store_scattered_kernel(
 
         xt_p = plane_tile("xt_p", T, 0)
         w_p = plane_tile("w_p", R, 64)
-        xo_p = plane_tile("xo_p", T, 64)
         w0_p = plane_tile("w0_p", R, 0)
+        xo_p = plane_tile("xo_p", T, 64)
         vs_p = tile("vs_p", [P, T], U8)
         nc.vector.memset(vs_p[:].bitcast(I32), 0)
-        pages = [tile("page%d" % i, [P, E], F32) for i in range(2)]
-        for page in pages:
-            nc.vector.memset(page[:], 0.0)
 
+        sa_t = tile("sa_t", [P, PACK], F32)
+        nc.gpsimd.dma_start(sa_t[:], sa.rearrange("(p t) o -> p (t o)", t=PACK))
         load_list("offs", offs)
-        xt_w = load_words(nc.sync, "xt_w", xt_words[0], T, U16)
-        w_w = load_words(nc.sync, "w_w", w_words[0].rearrange("p c r -> p (c r)"), R, U32)
-        xo_w = load_words(nc.sync, "xo_w", xo_words[0].rearrange("p c r -> p (c r)"), T, U32)
-        load_plane(nc.scalar, xt_p, xt_scales, 0)
-        load_plane(nc.scalar, w_p, w_scales, 64)
+        xt_w = load_words(nc.scalar, "xt_w", xt_words[0], T, U16)
+        load_plane(nc.sync, xt_p, xt_scales, 0, 0)
+        w_w = load_words(nc.scalar, "w_w", w_words[0].rearrange("p c r -> p (c r)"), R, U32)
+        load_plane(nc.sync, xt_p, xt_scales, 0, 1)
+        load_plane(nc.scalar, w_p, w_scales, 64, 0)
+        load_plane(nc.sync, w_p, w_scales, 64, 1)
+        xo_w = load_words(nc.scalar, "xo_w", xo_words[0].rearrange("p c r -> p (c r)"), T, U32)
         load_list("offs2", offs2)
+        for q in range(2):
+            load_plane(nc.sync, w0_p, w0_scales, 0, q)
+            load_plane(nc.sync, xo_p, xo_scales, 64, q)
         w0_w = load_words(nc.sync, "w0_w", w0_words[0], R, U16)
         load_list("offs4", offs4)
         vs_w = load_words(nc.sync, "vs_w", vs_words[0], T, U16)
-        load_plane(nc.scalar, xo_p, xo_scales, 64)
-        load_plane(nc.scalar, w0_p, w0_scales, 0)
         load_list("offs3", offs3)
-        sa_t = tile("sa_t", [P, PACK], F32)
-        nc.sync.dma_start(sa_t[:], sa.rearrange("(p t) o -> p (t o)", t=PACK))
         vs_rows = vs_scales[0].bitcast(I32)
         for q in range(4):
             nc.sync.dma_start(vs_p[:].bitcast(I32)[32 * q : 32 * q + 4, :], vs_rows[4 * q : 4 * q + 4, :])
@@ -110,9 +109,13 @@ def tile_list_lessneighbour_bank_store_scattered_kernel(
 
         def deal(engine_copy, name, src, dtype):
             d = tile(name, [P, PACK, P], dtype)
+            order = "p m t" if dtype == U32 else "p t m"
             view = src.rearrange("p (m t) -> p t m", t=PACK)
             for t in range(0, PACK, 2):
-                engine_copy(d[:, t : t + 2, :], view[:, t : t + 2, :])
+                engine_copy(
+                    d[:, t : t + 2, :].rearrange("p t m -> " + order),
+                    view[:, t : t + 2, :].rearrange("p t m -> " + order),
+                )
             return d
 
         acc = [ps.tile([P, J], F32, name="acc%d" % t) for t in range(PACK)]
@@ -141,47 +144,56 @@ def tile_list_lessneighbour_bank_store_scattered_kernel(
                 rhs=xo_g[:].bitcast(E4M3), rhs_scale=xo_gs[:], start=False, stop=True,
             )
 
-        vs_g = gather("vs_g", vs_w[:], lists["offs4"], U16)
+        pages = [tile("page0", [P, E], F32, tag="w0_p"), tile("page1", [P, E], F32, tag="xo_p")]
+        for page in reversed(pages):
+            for c in range(0, E, E // 2):
+                nc.gpsimd.memset(page[:, c : c + E // 2], 0.0)
 
         a = []
         for t in range(PACK):
             a.append(tile("a%d" % t, [P, J], F32))
-            nc.vector.tensor_copy(a[t][:], acc[t][:])
+            (nc.scalar.copy if t < 2 else nc.vector.tensor_copy)(a[t][:], acc[t][:])
+        vs_g = gather("vs_g", vs_w[:], lists["offs4"], U16)
+        vs_gs = gather("vs_gs", vs_p[:], lists["offs4"], U8)
 
-        diffs = []
-        for h in range(2):
+        def differences(h):
             part = lists["offs3"][:, 8 * h : 8 * h + 8]
-            diff = tile("diff%d" % h, [P, PACK, HALF], F32)
+            diff = tile("diff%d" % h, [P, PACK, HALF], F32, tag="vs_p" if h == 0 else "g0_3")
             for t in range(PACK):
                 g = tile("g%d_%d" % (h, t), [P, HALF], F32)
                 nc.scalar.activation(out=g[:], in_=a[t][:].indirect(part), func=ACT.Copy, scale=sa_t[:, t : t + 1])
                 nc.vector.tensor_tensor(diff[:, t, :], acc[t][:, HALF * h : HALF * (h + 1)], g[:], ALU.subtract)
-            diffs.append(diff)
-            if h == 0:
-                vs_gs = gather("vs_gs", vs_p[:], lists["offs4"], U8)
+            return diff[:].rearrange("p t j -> p j t")
 
-        hids = []
-        for h in range(2):
-            hid = tile("hid%d" % h, [P, HALF, PACK], BF16)
-            nc.scalar.activation(out=hid[:], in_=diffs[h][:].rearrange("p t j -> p j t"), func=ACT.Abs)
-            hids.append(hid)
-
-        for h in range(2):
+        def products(h, hid):
             hq = tile("hq%d" % h, [P, HALF], U32)
             hs = tile("hs%d" % h, [P, HALF], U8)
-            nc.vector.quantize_mx(out=hq[:].bitcast(E5M2), scales=hs[:], in_=hids[h][:].rearrange("p j t -> p (j t)"))
-            part = lists["offs5"][:, 8 * h : 8 * h + 8]
-            res = []
+            nc.vector.quantize_mx(out=hq[:].bitcast(E5M2), scales=hs[:], in_=hid[:].rearrange("p j t -> p (j t)"))
+            prods = {}
             for i in (1, 0):
-                prod = ps.tile([P, HALF], F32, name="prod%d_%d" % (h, i))
+                prods[i] = ps.tile([P, HALF], F32, name="prod%d_%d" % (h, i))
                 nc.tensor.matmul_mx(
-                    out=prod[:], lhsT=vs_g[:, P * i : P * (i + 1)].bitcast(E2M1), lhsT_scale=vs_gs[:, P * i : P * (i + 1)],
+                    out=prods[i][:], lhsT=vs_g[:, P * i : P * (i + 1)].bitcast(E2M1),
+                    lhsT_scale=vs_gs[:, P * i : P * (i + 1)],
                     rhs=hq[:].bitcast(E5M2), rhs_scale=hs[:], start=True, stop=True,
                 )
-                res.append(tile("res%d_%d" % (h, i), [P, HALF], F32))
-                nc.vector.tensor_copy(res[-1][:], prod[:])
-            nc.scalar.activation(out=pages[1][:].indirect(part), in_=res[0][:], func=ACT.Copy)
-            nc.vector.tensor_copy(pages[0][:].indirect(part), res[1][:])
+            return prods
+
+        def place(h, prods, copy1):
+            part = lists["offs5"][:, 8 * h : 8 * h + 8]
+            res = [tile("res%d_%d" % (h, i), [P, HALF], F32) for i in range(2)]
+            copy1(res[1][:], prods[1][:])
+            nc.scalar.activation(out=pages[1][:].indirect(part), in_=res[1][:], func=ACT.Copy)
+            nc.vector.tensor_copy(res[0][:], prods[0][:])
+            nc.vector.tensor_copy(pages[0][:].indirect(part), res[0][:])
+
+        hids = [tile("hid%d" % h, [P, HALF, PACK], BF16) for h in range(2)]
+        diffs = [differences(h) for h in range(2)]
+        for h in range(2):
+            nc.scalar.activation(out=hids[h][:], in_=diffs[h], func=ACT.Abs)
+        prods = [products(h, hids[h]) for h in range(2)]
+        for h in range(2):
+            place(h, prods[h], nc.scalar.copy)
 
         nc.sync.dma_start(out[0:P, :], pages[0][:])
         nc.scalar.dma_start(out[P : 2 * P, :], pages[1][:])

@@ -77,34 +77,40 @@ def tile_list_lessneighbour_bank_store_scattered_kernel(
             nc.vector.tensor_copy(g[:], window.indirect(idx[:]))
             return g
 
-        xt_p = plane_tile("xt_p", T, 0)
-        w_p = plane_tile("w_p", R, 64)
-        w0_p = plane_tile("w0_p", R, 0)
-        xo_p = plane_tile("xo_p", T, 64)
-        vs_p = tile("vs_p", [P, T], U8)
-        nc.vector.memset(vs_p[:].bitcast(I32), 0)
+        def direct_plane(name):
+            t = tile(name, [P, T], U8)
+            nc.vector.memset(t[:].bitcast(I32), 0)
+            return t
 
+        def load_direct(t, src):
+            rows = src[0].bitcast(I32)
+            for q in range(4):
+                nc.sync.dma_start(t[:].bitcast(I32)[32 * q : 32 * q + 4, :], rows[4 * q : 4 * q + 4, :])
+
+        w_p = plane_tile("w_p", R, 64)
+        xt_p = plane_tile("xt_p", T, 0)
+        w0_p = plane_tile("w0_p", R, 0)
+        xo_p = direct_plane("xo_p")
+        vs_p = direct_plane("vs_p")
+
+        w0_w = load_words(nc.gpsimd, "w0_w", w0_words[0], R, U16)
         sa_t = tile("sa_t", [P, PACK], F32)
         nc.gpsimd.dma_start(sa_t[:], sa.rearrange("(p t) o -> p (t o)", t=PACK))
         load_list("offs", offs)
         xt_w = load_words(nc.scalar, "xt_w", xt_words[0], T, U16)
-        load_plane(nc.sync, xt_p, xt_scales, 0, 0)
-        w_w = load_words(nc.scalar, "w_w", w_words[0].rearrange("p c r -> p (c r)"), R, U32)
-        load_plane(nc.sync, xt_p, xt_scales, 0, 1)
-        load_plane(nc.scalar, w_p, w_scales, 64, 0)
-        load_plane(nc.sync, w_p, w_scales, 64, 1)
-        xo_w = load_words(nc.scalar, "xo_w", xo_words[0].rearrange("p c r -> p (c r)"), T, U32)
+        w_w = load_words(nc.sync, "w_w", w_words[0].rearrange("p c r -> p (c r)"), R, U32)
+        for q in range(2):
+            load_plane(nc.scalar, w_p, w_scales, 64, q)
+            load_plane(nc.sync, xt_p, xt_scales, 0, q)
+        xo_w = load_words(nc.sync, "xo_w", xo_words[0].rearrange("p c r -> p (c r)"), T, U32)
         load_list("offs2", offs2)
         for q in range(2):
             load_plane(nc.sync, w0_p, w0_scales, 0, q)
-            load_plane(nc.sync, xo_p, xo_scales, 64, q)
-        w0_w = load_words(nc.sync, "w0_w", w0_words[0], R, U16)
+        load_direct(xo_p, xo_scales)
+        load_list("offs3", offs3)
         load_list("offs4", offs4)
         vs_w = load_words(nc.sync, "vs_w", vs_words[0], T, U16)
-        load_list("offs3", offs3)
-        vs_rows = vs_scales[0].bitcast(I32)
-        for q in range(4):
-            nc.sync.dma_start(vs_p[:].bitcast(I32)[32 * q : 32 * q + 4, :], vs_rows[4 * q : 4 * q + 4, :])
+        load_direct(vs_p, vs_scales)
         load_list("offs5", offs5)
 
         def deal(engine_copy, name, src, dtype):
@@ -120,8 +126,8 @@ def tile_list_lessneighbour_bank_store_scattered_kernel(
 
         acc = [ps.tile([P, J], F32, name="acc%d" % t) for t in range(PACK)]
 
-        xt_win = window_plane("xt_win", xt_p, T, 0)
         w_win = fold_plane(w_p, R, 64)
+        xt_win = window_plane("xt_win", xt_p, T, 0)
         w_sd = deal(nc.gpsimd.tensor_copy, "w_sd", w_win, U8)
         w_d = deal(nc.scalar.copy, "w_d", w_w[:], U32)
         xt_gs = gather("xt_gs", xt_win, lists["offs"], U8)
@@ -134,10 +140,9 @@ def tile_list_lessneighbour_bank_store_scattered_kernel(
 
         xo_g = gather("xo_g", xo_w[:], lists["offs2"], U32)
         w0_win = fold_plane(w0_p, R, 0)
-        xo_win = window_plane("xo_win", xo_p, T, 64)
         w0_sd = deal(nc.gpsimd.tensor_copy, "w0_sd", w0_win, U8)
         w0_d = deal(nc.scalar.copy, "w0_d", w0_w[:], U16)
-        xo_gs = gather("xo_gs", xo_win, lists["offs2"], U8)
+        xo_gs = gather("xo_gs", xo_p[:], lists["offs2"], U8)
         for t in range(PACK):
             nc.tensor.matmul_mx(
                 out=acc[t][:], lhsT=w0_d[:, t, :].bitcast(E2M1), lhsT_scale=w0_sd[:, t, :],

@@ -168,7 +168,7 @@ def tile_list_lessneighbour_bank_store_scattered_kernel(
                 g = tile("g%d_%d" % (h, t), [P, HALF], F32)
                 nc.scalar.activation(out=g[:], in_=a[t][:].indirect(part), func=ACT.Copy, scale=sa_t[:, t : t + 1])
                 nc.vector.tensor_tensor(diff[:, t, :], acc[t][:, HALF * h : HALF * (h + 1)], g[:], ALU.subtract)
-            return diff[:].rearrange("p t j -> p j t")
+            return diff[:].rearrange("p t (c i) -> p c t i", i=4)
 
         def products(h, hid):
             hq = tile("hq%d" % h, [P, HALF], U32)
@@ -195,7 +195,7 @@ def tile_list_lessneighbour_bank_store_scattered_kernel(
         hids = [tile("hid%d" % h, [P, HALF, PACK], BF16) for h in range(2)]
         diffs = [differences(h) for h in range(2)]
         for h in range(2):
-            nc.scalar.activation(out=hids[h][:], in_=diffs[h], func=ACT.Abs)
+            nc.scalar.activation(out=hids[h][:].rearrange("p (c i) t -> p c t i", i=4), in_=diffs[h], func=ACT.Abs)
         prods = [products(h, hids[h]) for h in range(2)]
         for h in range(2):
             place(h, prods[h], nc.scalar.copy)

from contextlib import ExitStack

import concourse.mybir as mybir

K, T, J, R, N, E = 512, 1024, 256, 512, 256, 1024
FLOPS = 2 * (2 * K * R * J + R * N * J)

F32 = mybir.dt.float32
BF16 = mybir.dt.bfloat16
I32 = mybir.dt.int32
U32 = mybir.dt.uint32
U16 = mybir.dt.uint16
U8 = mybir.dt.uint8
E4M3 = mybir.dt.float8_e4m3fn_x4
E5M2 = mybir.dt.float8_e5m2_x4
E2M1 = mybir.dt.float4_e2m1fn_x4
ACT = mybir.ActivationFunctionType
ALU = mybir.AluOpType

P = 128
PACK = 4
HALF = J // 2


def tile_list_lessneighbour_bank_store_scattered_kernel(
    tc, xt_words, xt_scales, w_words, w_scales, xo_words, xo_scales, w0_words, w0_scales, sa,
    vs_words, vs_scales, offs, offs2, offs3, offs4, offs5, out,
):
    nc = tc.nc
    with ExitStack() as ctx:
        sb = ctx.enter_context(tc.tile_pool(name="sb", bufs=1))
        ps = ctx.enter_context(tc.psum_pool(name="ps", bufs=1))

        def tile(name, shape, dtype, tag=None):
            return sb.tile(shape, dtype, name=name, tag=tag or name, align_bytes=64)

        lists = {}

        def load_list(name, src):
            lists[name] = tile(name, [P, J // 16], U16)
            nc.sync.dma_start(lists[name][:], src)

        def load_words(queue, name, src, cols, dtype):
            t = tile(name, [P, cols], dtype)
            queue.dma_start(t[:].bitcast(I32), src.bitcast(I32))
            return t

        def plane_tile(name, cols, base):
            t = tile(name, [P, 2 * cols], U8)
            nc.vector.memset(t[:].bitcast(I32)[base : base + 64, :], 0)
            return t

        def load_plane(queue, t, src, base, q):
            rows = src[0].bitcast(I32).rearrange("(b q r) n -> q r b n", b=2, q=2)
            dst = t[:].bitcast(I32)[base + 32 * q : base + 32 * q + 4, :]
            queue.dma_start(dst.rearrange("p (b n) -> p b n", b=2), rows[q])

        def fold_plane(t, cols, base):
            t32 = t[:].bitcast(I32)
            c = cols // 4
            if base == 0:
                nc.vector.tensor_copy(t32[64:128, 0:c], t32[0:64, c : 2 * c])
                return t[:, 0:cols]
            nc.vector.tensor_copy(t32[0:64, c : 2 * c], t32[64:128, 0:c])
            return t[:, cols : 2 * cols]

        def window_plane(name, t, cols, base):
            win = tile(name, [P, cols], U8)
            t32, w32 = t[:].bitcast(I32), win[:].bitcast(I32)
            c = cols // 4
            for b in range(2):
                nc.vector.tensor_copy(w32[64 * b : 64 * b + 64, :], t32[base : base + 64, c * b : c * (b + 1)])
            return win[:]

        def gather(name, window, idx, dtype):
            g = tile(name, [P, J], dtype)
            nc.vector.tensor_copy(g[:], window.indirect(idx[:]))
            return g

        def direct_plane(name):
            t = tile(name, [P, T], U8)
            nc.vector.memset(t[:].bitcast(I32), 0)
            return t

        def load_direct(t, src):
            rows = src[0].bitcast(I32)
            for q in range(4):
                nc.sync.dma_start(t[:].bitcast(I32)[32 * q : 32 * q + 4, :], rows[4 * q : 4 * q + 4, :])

        w_p = plane_tile("w_p", R, 64)
        xt_p = plane_tile("xt_p", T, 0)
        w0_p = plane_tile("w0_p", R, 0)
        xo_p = direct_plane("xo_p")
        vs_p = direct_plane("vs_p")

        w0_w = load_words(nc.gpsimd, "w0_w", w0_words[0], R, U16)
        sa_t = tile("sa_t", [P, PACK], F32)
        nc.gpsimd.dma_start(sa_t[:], sa.rearrange("(p t) o -> p (t o)", t=PACK))
        load_list("offs", offs)
        xt_w = load_words(nc.scalar, "xt_w", xt_words[0], T, U16)
        w_w = load_words(nc.sync, "w_w", w_words[0].rearrange("p c r -> p (c r)"), R, U32)
        for q in range(2):
            load_plane(nc.scalar, w_p, w_scales, 64, q)
            load_plane(nc.sync, xt_p, xt_scales, 0, q)
        xo_w = load_words(nc.sync, "xo_w", xo_words[0].rearrange("p c r -> p (c r)"), T, U32)
        load_list("offs2", offs2)
        for q in range(2):
            load_plane(nc.sync, w0_p, w0_scales, 0, q)
        load_direct(xo_p, xo_scales)
        load_list("offs3", offs3)
        load_list("offs4", offs4)
        vs_w = load_words(nc.sync, "vs_w", vs_words[0], T, U16)
        load_direct(vs_p, vs_scales)
        load_list("offs5", offs5)

        def deal(engine_copy, name, src, dtype):
            d = tile(name, [P, PACK, P], dtype)
            order = "p m t" if dtype == U32 else "p t m"
            view = src.rearrange("p (m t) -> p t m", t=PACK)
            for t in range(0, PACK, 2):
                engine_copy(
                    d[:, t : t + 2, :].rearrange("p t m -> " + order),
                    view[:, t : t + 2, :].rearrange("p t m -> " + order),
                )
            return d

        acc = [ps.tile([P, J], F32, name="acc%d" % t) for t in range(PACK)]

        w_win = fold_plane(w_p, R, 64)
        xt_win = window_plane("xt_win", xt_p, T, 0)
        w_sd = deal(nc.gpsimd.tensor_copy, "w_sd", w_win, U8)
        w_d = deal(nc.scalar.copy, "w_d", w_w[:], U32)
        xt_gs = gather("xt_gs", xt_win, lists["offs"], U8)
        xt_g = gather("xt_g", xt_w[:], lists["offs"], U16)
        for t in range(PACK):
            nc.tensor.matmul_mx(
                out=acc[t][:], lhsT=w_d[:, t, :].bitcast(E4M3), lhsT_scale=w_sd[:, t, :],
                rhs=xt_g[:].bitcast(E2M1), rhs_scale=xt_gs[:], start=True, stop=False,
            )

        xo_g = gather("xo_g", xo_w[:], lists["offs2"], U32)
        w0_win = fold_plane(w0_p, R, 0)
        w0_sd = deal(nc.gpsimd.tensor_copy, "w0_sd", w0_win, U8)
        w0_d = deal(nc.scalar.copy, "w0_d", w0_w[:], U16)
        xo_gs = gather("xo_gs", xo_p[:], lists["offs2"], U8)
        for t in range(PACK):
            nc.tensor.matmul_mx(
                out=acc[t][:], lhsT=w0_d[:, t, :].bitcast(E2M1), lhsT_scale=w0_sd[:, t, :],
                rhs=xo_g[:].bitcast(E4M3), rhs_scale=xo_gs[:], start=False, stop=True,
            )

        pages = [tile("page0", [P, E], F32, tag="w0_p"), tile("page1", [P, E], F32, tag="xo_p")]
        for page in reversed(pages):
            for c in range(0, E, E // 2):
                nc.gpsimd.memset(page[:, c : c + E // 2], 0.0)

        a = []
        for t in range(PACK):
            a.append(tile("a%d" % t, [P, J], F32))
            (nc.scalar.copy if t < 2 else nc.vector.tensor_copy)(a[t][:], acc[t][:])
        vs_g = gather("vs_g", vs_w[:], lists["offs4"], U16)
        vs_gs = gather("vs_gs", vs_p[:], lists["offs4"], U8)

        def differences(h):
            part = lists["offs3"][:, 8 * h : 8 * h + 8]
            diff = tile("diff%d" % h, [P, PACK, HALF], F32, tag="vs_p" if h == 0 else "g0_3")
            for t in range(PACK):
                g = tile("g%d_%d" % (h, t), [P, HALF], F32)
                nc.scalar.activation(out=g[:], in_=a[t][:].indirect(part), func=ACT.Copy, scale=sa_t[:, t : t + 1])
                nc.vector.tensor_tensor(diff[:, t, :], acc[t][:, HALF * h : HALF * (h + 1)], g[:], ALU.subtract)
            return diff[:].rearrange("p t (c i) -> p c t i", i=4)

        def products(h, hid):
            hq = tile("hq%d" % h, [P, HALF], U32)
            hs = tile("hs%d" % h, [P, HALF], U8)
            nc.vector.quantize_mx(out=hq[:].bitcast(E5M2), scales=hs[:], in_=hid[:].rearrange("p j t -> p (j t)"))
            prods = {}
            for i in (1, 0):
                prods[i] = ps.tile([P, HALF], F32, name="prod%d_%d" % (h, i))
                nc.tensor.matmul_mx(
                    out=prods[i][:], lhsT=vs_g[:, P * i : P * (i + 1)].bitcast(E2M1),
                    lhsT_scale=vs_gs[:, P * i : P * (i + 1)],
                    rhs=hq[:].bitcast(E5M2), rhs_scale=hs[:], start=True, stop=True,
                )
            return prods

        def place(h, prods, copy1):
            part = lists["offs5"][:, 8 * h : 8 * h + 8]
            res = [tile("res%d_%d" % (h, i), [P, HALF], F32) for i in range(2)]
            copy1(res[1][:], prods[1][:])
            nc.scalar.activation(out=pages[1][:].indirect(part), in_=res[1][:], func=ACT.Copy)
            nc.vector.tensor_copy(res[0][:], prods[0][:])
            nc.vector.tensor_copy(pages[0][:].indirect(part), res[0][:])

        hids = [tile("hid%d" % h, [P, HALF, PACK], BF16) for h in range(2)]
        diffs = [differences(h) for h in range(2)]
        for h in range(2):
            nc.scalar.activation(out=hids[h][:].rearrange("p (c i) t -> p c t i", i=4), in_=diffs[h], func=ACT.Abs)
        prods = [products(h, hids[h]) for h in range(2)]
        for h in range(2):
            place(h, prods[h], nc.scalar.copy)

        nc.sync.dma_start(out[0:P, :], pages[0][:])
        nc.scalar.dma_start(out[P : 2 * P, :], pages[1][:])
